import numpy as np
import ml_dtypes


def mxq(x, axis, fmt="e4m3"):
    dtype, down = {"e4m3": (ml_dtypes.float8_e4m3fn, 7), "e5m2": (ml_dtypes.float8_e5m2, 14)}[fmt]
    v = np.moveaxis(np.asarray(x, np.float32).astype(ml_dtypes.bfloat16).astype(np.float64), axis, -1)
    blocks = v.reshape(v.shape[:-1] + (-1, 32))
    amax = np.abs(blocks).max(-1, keepdims=True)
    byte = np.maximum(np.where(amax > 0, np.frexp(amax)[1] - 1 + 127, 0) - down, 1)
    scale = np.exp2(byte - 127.0)
    codes = (blocks / scale).astype(np.float32).astype(dtype).astype(np.float64)
    return np.moveaxis((codes * scale).reshape(v.shape), -1, axis)


WIDE = False


def mx_kscale(k):
    if not WIDE:
        return np.ones(k)
    levels = np.array([10, -10, 5, -5, 0])
    if k % 512:
        return np.exp2(np.random.permutation(np.resize(levels, k // 32))).repeat(32)
    a = np.empty((k // 512, 16))
    for p in range(k // 512):
        a[p, :8] = np.random.permutation(np.resize(levels, 8))
        for g in range(8):
            far = levels[np.abs(levels - a[p, g]) >= 10]
            a[p, g + 8] = far[np.random.randint(len(far))]
    return np.exp2(a.ravel()).repeat(32)


BF16 = ml_dtypes.bfloat16


def bf(x):
    return np.asarray(x, np.float32).astype(BF16)


def f64(x):
    return np.asarray(x).astype(np.float64)


N, D, L, K, O = 128, 2048, 3072, 3, 2048


def smooth_reciprocal(z):
    return z / (z * z + 0.5)


def draw0():
    s, t = mx_kscale(D), mx_kscale(L)
    return {
        "x": bf(np.random.standard_normal((N, D)) * s),
        "w0": bf(np.random.standard_normal((D, L)) / np.sqrt(D) / s[:, None]),
        "w1": bf(np.random.standard_normal((D, L)) / np.sqrt(D) / s[:, None]),
        "w2": bf(np.random.standard_normal((D, L)) / np.sqrt(D) / s[:, None]),
        "b": bf(0.3 * np.random.standard_normal((K, L))),
        "g": bf((1.0 + 0.1 * np.random.standard_normal(L)) * t),
        "v": bf(np.random.standard_normal((L, O)) / np.sqrt(L) / t[:, None]),
    }


def core(x, w0, w1, w2, b, g, v):
    b = f64(b)
    xq = mxq(f64(x), 1, "e4m3")
    a0 = (xq @ mxq(f64(w0), 0, "e4m3")) + b[0]
    a1 = (xq @ mxq(f64(w1), 0, "e4m3")) + b[1]
    a2 = (xq @ mxq(f64(w2), 0, "e4m3")) + b[2]
    f1 = a1 + smooth_reciprocal(a2)
    f0 = a0 + smooth_reciprocal(f1)
    h = f0 * f64(g)[None, :]
    return mxq(h, 1, "e4m3") @ mxq(f64(v), 0, "e4m3")


def e4m3fn_bytes(y):
    return np.clip(np.asarray(y, np.float64), -448.0, 448.0).astype(np.float32).astype(ml_dtypes.float8_e4m3fn).view(np.uint8)


def e4m3fn_values(b):
    return np.asarray(b, np.uint8).view(ml_dtypes.float8_e4m3fn).astype(np.float64)


def setup_inputs():
    d = draw0()
    x0 = np.asarray(d['w2']).astype(np.float64)
    s = (np.max(np.abs(x0), axis=(1,), keepdims=True) / 448.0).astype(np.float32)
    out = {}
    for k, v in d.items():
        if k == 'w2':
            out['w2_bytes'] = e4m3fn_bytes(x0 / s.astype(np.float64))
            out['w2_scale'] = s
        else:
            out[k] = v
    return out


def reference(x, w0, w1, w2_bytes, w2_scale, b, g, v):
    return core(x, w0, w1, e4m3fn_values(w2_bytes) * w2_scale.astype(np.float64), b, g, v)

@@ -1,0 +1,357 @@
+from contextlib import ExitStack
+
+import concourse.mybir as mybir
+from concourse.masks import make_identity
+
+N, D, L, O = 128, 2048, 3072, 2048
+
+F32 = mybir.dt.float32
+BF16 = mybir.dt.bfloat16
+U32 = mybir.dt.uint32
+U8 = mybir.dt.uint8
+FP8 = mybir.dt.float8_e4m3fn
+FP8X4 = mybir.dt.float8_e4m3fn_x4
+ALU = mybir.AluOpType
+ACT = mybir.ActivationFunctionType
+
+FLOPS = 2 * N * D * L * 3 + 2 * N * L * O
+
+P = 128
+J = 4
+W = 1024
+PASSES = D // 512
+RANGES = L // W
+HALVES = O // W
+GROUPS = L // 512
+Q = W // 16
+
+LOAD_LEAD = 5
+RAW_BUFS = 6
+WIDE_LEAD = 3
+S_LEAD = 2
+TURN_LEAD = 3
+X_STEP = 0
+LAGS = (1, 3, 4, 6, 7, 9, 10)
+ORDER = [(1, 0), (2, 0), (1, 1), (1, 2), (2, 1), (1, 3), (0, 0), (2, 2), (0, 1), (0, 2), (2, 3), (0, 3)]
+ENGINES = ["VVVSVVSVVVVS", "VVVSVVSVVSVV", "VVVSVVSVVSVV", "TVSVTVSVTVVT"]
+
+
+def tile_cofrnetladderlayer_w_kernel(tc, x, w0, w1, w2_bytes, w2_scale, b, g, v, out):
+    nc = tc.nc
+    with ExitStack() as ctx:
+        keep = ctx.enter_context(tc.tile_pool(name="keep", bufs=1))
+        raws = ctx.enter_context(tc.tile_pool(name="raws", bufs=RAW_BUFS))
+        raw8s = ctx.enter_context(tc.tile_pool(name="raw8s", bufs=4))
+        wides = ctx.enter_context(tc.tile_pool(name="wides", bufs=2))
+        grps = ctx.enter_context(tc.tile_pool(name="grps", bufs=4))
+        qs = ctx.enter_context(tc.tile_pool(name="qs", bufs=12))
+        ep = ctx.enter_context(tc.tile_pool(name="ep", bufs=2))
+        psum = ctx.enter_context(tc.psum_pool(name="psum", bufs=8))
+        ctx.enter_context(tc.manual_schedule())
+
+        warm = keep.tile([P, 1], F32)
+        half = keep.tile([P, 1], F32)
+        nc.vector.memset(half[:], 0.5)
+        nc.scalar.activation(out=warm[:], in_=half[:], func=ACT.Abs_reciprocal_sqrt)
+        rows = keep.tile([P, 512], BF16)
+        nc.vector.memset(rows[:], 0.0)
+        ident32 = keep.tile([P, P], F32)
+        make_identity(nc, ident32[:])
+        ident16 = keep.tile([P, P], BF16)
+        make_identity(nc, ident16[:])
+
+        x_sb = keep.tile([P, D], BF16)
+        scale = keep.tile([P, PASSES, J], F32)
+
+        units = []
+        for r in range(RANGES):
+            for i, (m, p) in enumerate(ORDER):
+                units.append({"mat": m, "pass": p, "col": r, "engine": ENGINES[r][i]})
+        for hh in range(HALVES):
+            for p in range(GROUPS):
+                units.append({"mat": 3, "pass": p, "col": hh, "engine": ENGINES[3][6 * hh + p]})
+        total = len(units)
+
+        def load(u):
+            cols = slice(u["col"] * W, (u["col"] + 1) * W)
+            p = u["pass"]
+            if u["mat"] == 2:
+                raw8 = raw8s.tile([P, J, W], U8, name="raw8")
+                nc.sync.dma_start(
+                    out=raw8[:], in_=w2_bytes[p * 512:(p + 1) * 512, cols].rearrange("(p k) c -> p k c", k=J))
+                u["raw8"] = raw8
+                return
+            raw = raws.tile([P, J, W], BF16, name="raw")
+            u["raw"] = raw
+            if u["mat"] == 3:
+                vrows = v[p * 512:(p + 1) * 512, cols].rearrange("(q t i) c -> i q t c", t=J, i=4)
+                for i in range(4):
+                    nc.sync.dma_start(out=raw[i::4, :, :], in_=vrows[i])
+                return
+            w = w1 if u["mat"] == 1 else w0
+            nc.sync.dma_start(out=raw[:], in_=w[p * 512:(p + 1) * 512, cols].rearrange("(p k) c -> p k c", k=J))
+
+        def widen(u):
+            wide = wides.tile([P, J, W], BF16, name="wide")
+            for k in range(J):
+                nc.scalar.activation(
+                    out=wide[:, k, :], in_=u["raw8"][:, k, :].bitcast(FP8), func=ACT.Copy,
+                    scale=scale[:, u["pass"], k:k + 1])
+            u["raw"] = wide
+
+        def turn(u, s):
+            bank = psum.tile([P, 256, J], BF16, name="bank")
+            u["banks"] = u.get("banks", []) + [bank]
+            for h2 in range(2):
+                c0 = 256 * s + 128 * h2
+                nc.tensor.matmul(
+                    bank[:, 128 * h2:128 * (h2 + 1), :], lhsT=ident16[:],
+                    rhs=u["raw"][:, :, c0:c0 + 128].rearrange("p k c -> p c k"), start=True, stop=True)
+
+        def unload(u, s):
+            if s == 0:
+                u["grp"] = grps.tile([P, J * W], BF16, name="grp", align_bytes=64)
+            nc.scalar.copy(
+                out=u["grp"][:, 1024 * s:1024 * (s + 1)], in_=u["banks"][s][:].rearrange("p c k -> p (c k)"))
+
+        def interleave(u):
+            engine = u["engine"]
+            grp = grps.tile([P, J * W], BF16, name="grp", align_bytes=64)
+            u["grp"] = grp
+            if u["mat"] == 3:
+                dst = grp[:].rearrange("p (c i k) -> p c k i", i=4, k=J)
+                src = u["raw"][:].rearrange("p k (c i) -> p c k i", i=4)
+            else:
+                dst = grp[:].rearrange("p (t q i k) -> p t q k i", t=4, i=4, k=J)
+                src = u["raw"][:].rearrange("p k (q t i) -> p t q k i", t=4, i=4)
+            if engine == "S":
+                nc.scalar.copy(out=dst, in_=src)
+            else:
+                nc.vector.tensor_copy(out=dst, in_=src)
+
+        def quantize(u):
+            codes = qs.tile([P, W], U32, name="codes", align_bytes=64)
+            planes = qs.tile([P, W], U8, name="planes", align_bytes=64)
+            nc.vector.quantize_mx(out=codes[:].bitcast(FP8X4), scales=planes[:], in_=u["grp"][:])
+            u["q"] = (codes, planes)
+
+        words = x_sb[:].bitcast(F32)
+        x_grp = keep.tile([P, PASSES, N, J], BF16, align_bytes=64)
+        x_codes = keep.tile([P, PASSES, N], U32, align_bytes=64)
+        x_planes = keep.tile([P, PASSES, N], U8, align_bytes=64)
+
+        def prepare_x():
+            x_words = x_grp[:].rearrange("p g n j -> p (g n j)").bitcast(F32).rearrange(
+                "p (g n u) -> p g n u", g=PASSES, u=2)
+            for h2 in range(2):
+                bank = psum.tile([P, 2, 2, N], F32, name="bank")
+                for gg in range(2):
+                    for uu in range(2):
+                        base = 256 * (2 * h2 + gg)
+                        nc.tensor.transpose(bank[:, gg, uu, :], words[:, base + uu:base + 256:2], ident32[:])
+                nc.vector.tensor_copy(
+                    out=x_words[:, 2 * h2:2 * h2 + 2], in_=bank[:].rearrange("p g u n -> p g n u"))
+            nc.vector.quantize_mx(
+                out=x_codes[:].rearrange("p g n -> p (g n)").bitcast(FP8X4),
+                scales=x_planes[:].rearrange("p g n -> p (g n)"),
+                in_=x_grp[:].rearrange("p g n j -> p (g n j)"))
+
+        col = keep.tile([P, 4, 32], F32)
+        gb0 = keep.tile([P, 4, GROUPS], F32)
+        rows_t = keep.tile([P, 4, 128], BF16)
+
+        def load_rows():
+            nc.sync.dma_start(out=rows[0:18, :], in_=b.rearrange("k (g c) -> (k g) c", c=512))
+            nc.sync.dma_start(out=rows[18:24, :], in_=g.rearrange("(g c) -> g c", c=512))
+
+        def prepare_rows():
+            nc.vector.tensor_copy(
+                out=rows_t[:].rearrange("p t (q i) -> p t q i", i=4),
+                in_=rows[:].rearrange("p (q t i) -> p t q i", t=4, i=4))
+            bank = psum.tile([P, 4, 128], BF16, name="bank")
+            for t in range(4):
+                nc.tensor.transpose(bank[:, t, :], rows_t[:, t, :], ident16[:])
+            nc.vector.tensor_copy(out=col[:, :, 0:24], in_=bank[:, :, 0:24])
+            nc.vector.tensor_tensor(out=gb0[:], in0=col[:, :, 0:6], in1=col[:, :, 18:24], op=ALU.mult)
+
+        acc = {}
+        ready = {}
+
+        def first_matmuls(m, r):
+            mine = [u for u in units if u["mat"] == m and u["col"] == r]
+            mine.sort(key=lambda u: u["pass"])
+            for gl in range(2):
+                bank = psum.tile([P, 4, N], F32, name="bank")
+                acc[(m, 2 * r + gl)] = bank
+                for t in range(4):
+                    c0 = t * 256 + gl * 128
+                    for p in range(PASSES):
+                        codes, planes = mine[p]["q"]
+                        nc.tensor.matmul_mx(
+                            out=bank[:, t, :],
+                            lhsT=codes[:, c0:c0 + 128].bitcast(FP8X4), lhsT_scale=planes[:, c0:c0 + 128],
+                            rhs=x_codes[:, p, :].bitcast(FP8X4), rhs_scale=x_planes[:, p, :],
+                            start=(p == 0), stop=(p == PASSES - 1))
+
+        st = {}
+
+        def recip_half(src_sq, name):
+            y = ep.tile([P, 4, N], F32, name="y")
+            nc.scalar.activation(out=y[:], in_=src_sq[:], func=ACT.Abs_reciprocal_sqrt, bias=half[:])
+            rec = ep.tile([P, 4, N], F32, name="rec")
+            nc.scalar.activation(out=rec[:], in_=y[:], func=ACT.Square)
+            return rec
+
+        def e1_scalar(G):
+            sq = ep.tile([P, 4, N], F32, name="sq")
+            for t in range(4):
+                nc.scalar.activation(
+                    out=sq[:, t, :], in_=acc[(2, G)][:, t, :], func=ACT.Square, bias=col[:, t, 12 + G:13 + G])
+            st[("rec", G)] = recip_half(sq, "a")
+
+        def e1_vector(G):
+            r2 = ep.tile([P, 4, N], F32, name="r2")
+            for t in range(4):
+                nc.vector.scalar_tensor_tensor(
+                    out=r2[:, t, :], in0=acc[(2, G)][:, t, :], scalar=col[:, t, 12 + G:13 + G],
+                    in1=st[("rec", G)][:, t, :], op0=ALU.add, op1=ALU.mult)
+            st[("r2", G)] = r2
+
+        def e2_vector(G):
+            z1 = ep.tile([P, 4, N], F32, name="z1")
+            for t in range(4):
+                nc.vector.scalar_tensor_tensor(
+                    out=z1[:, t, :], in0=acc[(1, G)][:, t, :], scalar=col[:, t, 6 + G:7 + G],
+                    in1=st[("r2", G)][:, t, :], op0=ALU.add, op1=ALU.add)
+            st[("z1", G)] = z1
+
+        def e2_scalar(G):
+            sq = ep.tile([P, 4, N], F32, name="sq")
+            nc.scalar.activation(out=sq[:], in_=st[("z1", G)][:], func=ACT.Square)
+            st[("rec1", G)] = recip_half(sq, "b")
+
+        def e3_vector(G):
+            gr = ep.tile([P, 4, N], F32, name="gr")
+            for t in range(4):
+                nc.vector.scalar_tensor_tensor(
+                    out=gr[:, t, :], in0=st[("z1", G)][:, t, :], scalar=col[:, t, 18 + G:19 + G],
+                    in1=st[("rec1", G)][:, t, :], op0=ALU.mult, op1=ALU.mult)
+            st[("gr", G)] = gr
+
+        def e4_scalar(G):
+            z0 = ep.tile([P, 4, N], F32, name="z0")
+            for t in range(4):
+                nc.scalar.activation(
+                    out=z0[:, t, :], in_=acc[(0, G)][:, t, :], func=ACT.Identity,
+                    scale=col[:, t, 18 + G:19 + G], bias=gb0[:, t, G:G + 1])
+            st[("z0", G)] = z0
+
+        def e4_vector(G):
+            hb = ep.tile([P, N, 4], BF16, name="hb", align_bytes=64)
+            nc.vector.tensor_tensor(
+                out=hb[:], in0=st[("z0", G)][:].rearrange("p t n -> p n t"),
+                in1=st[("gr", G)][:].rearrange("p t n -> p n t"), op=ALU.add)
+            st[("hb", G)] = hb
+
+        h_codes = keep.tile([P, GROUPS, N], U32, align_bytes=64)
+        h_planes = keep.tile([P, GROUPS, N], U8, align_bytes=64)
+
+        def e5_vector(G):
+            nc.vector.quantize_mx(
+                out=h_codes[:, G, :].bitcast(FP8X4), scales=h_planes[:, G, :],
+                in_=st[("hb", G)][:].rearrange("p n t -> p (n t)"))
+
+        def last_matmuls(u):
+            hh, G = u["col"], u["pass"]
+            codes, planes = u["q"]
+            for s in range(2):
+                if G == 0:
+                    bank = psum.tile([P, 512], F32, name="bank")
+                    acc[("o", hh, s)] = bank
+                nc.tensor.matmul_mx(
+                    out=acc[("o", hh, s)][:],
+                    lhsT=h_codes[:, G, :].bitcast(FP8X4), lhsT_scale=h_planes[:, G, :],
+                    rhs=codes[:, 512 * s:512 * (s + 1)].bitcast(FP8X4), rhs_scale=planes[:, 512 * s:512 * (s + 1)],
+                    start=(G == 0), stop=(G == GROUPS - 1))
+
+        def finish(hh):
+            for s in range(2):
+                res = ep.tile([P, 512], F32, name="res")
+                if s == 0:
+                    nc.vector.tensor_copy(out=res[:], in_=acc[("o", hh, s)][:])
+                else:
+                    nc.scalar.copy(out=res[:], in_=acc[("o", hh, s)][:])
+                c0 = hh * W + s * 512
+                nc.sync.dma_start(out=out[:, c0:c0 + 512], in_=res[:])
+
+        later = {}
+
+        def at(step, fn, *args):
+            later.setdefault(step, []).append((fn, args))
+
+        def due(i, engine):
+            return 0 <= i < total and units[i]["engine"] == engine
+
+        done = {}
+        pending = []
+        ready_at = {}
+        for s in range(-LOAD_LEAD, total + 8):
+            if 0 <= s + LOAD_LEAD < total:
+                load(units[s + LOAD_LEAD])
+                if s + LOAD_LEAD == 1:
+                    nc.sync.dma_start(out=scale[:], in_=w2_scale.rearrange("(g p k) o -> p g (k o)", p=P, k=J))
+                    nc.sync.dma_start(out=x_sb[:], in_=x)
+                if s + LOAD_LEAD == 4:
+                    load_rows()
+            if s == X_STEP:
+                prepare_x()
+            if s == X_STEP + 2:
+                prepare_rows()
+            if due(s + TURN_LEAD, "T"):
+                for i in range(3):
+                    turn(units[s + TURN_LEAD], i)
+            if 0 <= s + WIDE_LEAD < total and units[s + WIDE_LEAD]["mat"] == 2:
+                widen(units[s + WIDE_LEAD])
+            if due(s + S_LEAD, "S"):
+                interleave(units[s + S_LEAD])
+            if due(s + TURN_LEAD - 1, "T"):
+                u = units[s + TURN_LEAD - 1]
+                unload(u, 0)
+                turn(u, 3)
+                for i in range(1, 4):
+                    unload(u, i)
+            if due(s + 1, "V"):
+                interleave(units[s + 1])
+            if 0 <= s < total:
+                u = units[s]
+                quantize(u)
+                m, r = u["mat"], u["col"]
+                done[(m, r)] = done.get((m, r), 0) + 1
+                if m == 3:
+                    pending.append(u)
+                elif done[(m, r)] == PASSES:
+                    first_matmuls(m, r)
+                    if m == 2:
+                        for gl in range(2):
+                            G = 2 * r + gl
+                            base = s + gl
+                            at(base + LAGS[0], e1_scalar, G)
+                            at(base + LAGS[1], e1_vector, G)
+                            at(base + LAGS[2], e2_vector, G)
+                            at(base + LAGS[2], e2_scalar, G)
+                            at(base + LAGS[3], e3_vector, G)
+                            at(base + LAGS[4], e4_scalar, G)
+                            at(base + LAGS[5], e4_vector, G)
+                            at(base + LAGS[6], e5_vector, G)
+                            ready_at[G] = base + LAGS[6]
+            for fn, args in later.get(s, []):
+                fn(*args)
+            rest = []
+            for u in pending:
+                if ready_at[u["pass"]] <= s and not rest:
+                    last_matmuls(u)
+                    if u["pass"] == GROUPS - 1:
+                        at(s + 1, finish, u["col"])
+                else:
+                    rest.append(u)
+            pending = rest

@@ -25,15 +25,16 @@ HALVES = O // W
 GROUPS = L // 512
 Q = W // 16
 
-LOAD_LEAD = 5
+LOAD_LEAD = 7
 RAW_BUFS = 6
-WIDE_LEAD = 3
+WIDE_LEAD = 5
 S_LEAD = 2
-TURN_LEAD = 3
+TURN_LEAD = 5
 X_STEP = 0
-LAGS = (1, 3, 4, 6, 7, 9, 10)
-ORDER = [(1, 0), (2, 0), (1, 1), (1, 2), (2, 1), (1, 3), (0, 0), (2, 2), (0, 1), (0, 2), (2, 3), (0, 3)]
-ENGINES = ["VVVSVVSVVVVS", "VVVSVVSVVSVV", "VVVSVVSVVSVV", "TVSVTVSVTVVT"]
+LAGS = (1, 4, 4, 6, 6, 8, 9)
+SHARES = {"V": 0, "a": 16, "b": 24, "c": 32, "S": 64}
+ORDER = [(0, 1), (2, 0), (0, 3), (1, 1), (2, 1), (0, 2), (1, 3), (2, 2), (0, 0), (1, 0), (2, 3), (1, 2)]
+ENGINES = ["aVbVVbbVbabb", "bcaVbcVabVaV", "bbbbbbVVcScV", "TbTbbcbbbTTc"]
 
 
 def tile_cofrnetladderlayer_w_kernel(tc, x, w0, w1, w2_bytes, w2_scale, b, g, v, out):
@@ -71,6 +72,10 @@ def tile_cofrnetladderlayer_w_kernel(tc, x, w0, w1, w2_bytes, w2_scale, b, g, v,
             for p in range(GROUPS):
                 units.append({"mat": 3, "pass": p, "col": hh, "engine": ENGINES[3][6 * hh + p]})
         total = len(units)
+        for u in units:
+            u["parts"] = [(0, W)]
+        for u in (units[0], units[-1]):
+            u["parts"] = [(0, W // 2), (W // 2, W)]
 
         def load(u):
             cols = slice(u["col"] * W, (u["col"] + 1) * W)
@@ -89,7 +94,9 @@ def tile_cofrnetladderlayer_w_kernel(tc, x, w0, w1, w2_bytes, w2_scale, b, g, v,
                     nc.sync.dma_start(out=raw[i::4, :, :], in_=vrows[i])
                 return
             w = w1 if u["mat"] == 1 else w0
-            nc.sync.dma_start(out=raw[:], in_=w[p * 512:(p + 1) * 512, cols].rearrange("(p k) c -> p k c", k=J))
+            src = w[p * 512:(p + 1) * 512, cols].rearrange("(p k) c -> p k c", k=J)
+            for c0, c1 in u["parts"]:
+                nc.sync.dma_start(out=raw[:, :, c0:c1], in_=src[:, :, c0:c1])
 
         def widen(u):
             wide = wides.tile([P, J, W], BF16, name="wide")
@@ -114,25 +121,32 @@ def tile_cofrnetladderlayer_w_kernel(tc, x, w0, w1, w2_bytes, w2_scale, b, g, v,
             nc.scalar.copy(
                 out=u["grp"][:, 1024 * s:1024 * (s + 1)], in_=u["banks"][s][:].rearrange("p c k -> p (c k)"))
 
-        def interleave(u):
-            engine = u["engine"]
-            grp = grps.tile([P, J * W], BF16, name="grp", align_bytes=64)
-            u["grp"] = grp
-            if u["mat"] == 3:
-                dst = grp[:].rearrange("p (c i k) -> p c k i", i=4, k=J)
-                src = u["raw"][:].rearrange("p k (c i) -> p c k i", i=4)
-            else:
-                dst = grp[:].rearrange("p (t q i k) -> p t q k i", t=4, i=4, k=J)
-                src = u["raw"][:].rearrange("p k (q t i) -> p t q k i", t=4, i=4)
-            if engine == "S":
-                nc.scalar.copy(out=dst, in_=src)
-            else:
-                nc.vector.tensor_copy(out=dst, in_=src)
+        def interleave(u, engine):
+            if "grp" not in u:
+                u["grp"] = grps.tile([P, J * W], BF16, name="grp", align_bytes=64)
+            grp = u["grp"]
+            edge = W - 16 * SHARES[u["engine"]]
+            for c0, c1 in u["parts"]:
+                if engine == "S":
+                    copy, c0, c1 = nc.scalar.copy, max(c0, edge), c1
+                else:
+                    copy, c0, c1 = nc.vector.tensor_copy, c0, min(c1, edge)
+                if c0 >= c1:
+                    continue
+                if u["mat"] == 3:
+                    dst = grp[:].rearrange("p (c i k) -> p c k i", i=4, k=J)[:, c0 // 4:c1 // 4]
+                    src = u["raw"][:].rearrange("p k (c i) -> p c k i", i=4)[:, c0 // 4:c1 // 4]
+                else:
+                    dst = grp[:].rearrange("p (t q i k) -> p t q k i", t=4, i=4, k=J)[:, :, c0 // 16:c1 // 16]
+                    src = u["raw"][:].rearrange("p k (q t i) -> p t q k i", t=4, i=4)[:, :, c0 // 16:c1 // 16]
+                copy(out=dst, in_=src)
 
         def quantize(u):
             codes = qs.tile([P, W], U32, name="codes", align_bytes=64)
             planes = qs.tile([P, W], U8, name="planes", align_bytes=64)
-            nc.vector.quantize_mx(out=codes[:].bitcast(FP8X4), scales=planes[:], in_=u["grp"][:])
+            for c0, c1 in (u["parts"] if u["mat"] == 3 else [(0, W)]):
+                nc.vector.quantize_mx(
+                    out=codes[:, c0:c1].bitcast(FP8X4), scales=planes[:, c0:c1], in_=u["grp"][:, J * c0:J * c1])
             u["q"] = (codes, planes)
 
         words = x_sb[:].bitcast(F32)
@@ -312,16 +326,16 @@ def tile_cofrnetladderlayer_w_kernel(tc, x, w0, w1, w2_bytes, w2_scale, b, g, v,
                     turn(units[s + TURN_LEAD], i)
             if 0 <= s + WIDE_LEAD < total and units[s + WIDE_LEAD]["mat"] == 2:
                 widen(units[s + WIDE_LEAD])
-            if due(s + S_LEAD, "S"):
-                interleave(units[s + S_LEAD])
+            if 0 <= s + S_LEAD < total and units[s + S_LEAD]["engine"] != "T":
+                interleave(units[s + S_LEAD], "S")
             if due(s + TURN_LEAD - 1, "T"):
                 u = units[s + TURN_LEAD - 1]
                 unload(u, 0)
                 turn(u, 3)
                 for i in range(1, 4):
                     unload(u, i)
-            if due(s + 1, "V"):
-                interleave(units[s + 1])
+            if 0 <= s + 1 < total and units[s + 1]["engine"] != "T":
+                interleave(units[s + 1], "V")
             if 0 <= s < total:
                 u = units[s]
                 quantize(u)

from contextlib import ExitStack

import concourse.mybir as mybir
from concourse.masks import make_identity

N, D, L, O = 128, 2048, 3072, 2048

F32 = mybir.dt.float32
BF16 = mybir.dt.bfloat16
U32 = mybir.dt.uint32
U8 = mybir.dt.uint8
FP8 = mybir.dt.float8_e4m3fn
FP8X4 = mybir.dt.float8_e4m3fn_x4
ALU = mybir.AluOpType
ACT = mybir.ActivationFunctionType

FLOPS = 2 * N * D * L * 3 + 2 * N * L * O

P = 128
J = 4
W = 1024
PASSES = D // 512
RANGES = L // W
HALVES = O // W
GROUPS = L // 512
Q = W // 16

LOAD_LEAD = 7
RAW_BUFS = 6
WIDE_LEAD = 5
S_LEAD = 2
TURN_LEAD = 5
X_STEP = 0
LAGS = (1, 4, 4, 6, 6, 8, 9)
SHARES = {"V": 0, "a": 16, "b": 24, "c": 32, "S": 64}
ORDER = [(0, 1), (2, 0), (0, 3), (1, 1), (2, 1), (0, 2), (1, 3), (2, 2), (0, 0), (1, 0), (2, 3), (1, 2)]
ENGINES = ["aVbVVbbVbabb", "bcaVbcVabVaV", "bbbbbbVVcScV", "TbTbbcbbbTTc"]


def tile_cofrnetladderlayer_w_kernel(tc, x, w0, w1, w2_bytes, w2_scale, b, g, v, out):
    nc = tc.nc
    with ExitStack() as ctx:
        keep = ctx.enter_context(tc.tile_pool(name="keep", bufs=1))
        raws = ctx.enter_context(tc.tile_pool(name="raws", bufs=RAW_BUFS))
        raw8s = ctx.enter_context(tc.tile_pool(name="raw8s", bufs=4))
        wides = ctx.enter_context(tc.tile_pool(name="wides", bufs=2))
        grps = ctx.enter_context(tc.tile_pool(name="grps", bufs=4))
        qs = ctx.enter_context(tc.tile_pool(name="qs", bufs=12))
        ep = ctx.enter_context(tc.tile_pool(name="ep", bufs=2))
        psum = ctx.enter_context(tc.psum_pool(name="psum", bufs=8))
        ctx.enter_context(tc.manual_schedule())

        warm = keep.tile([P, 1], F32)
        half = keep.tile([P, 1], F32)
        nc.vector.memset(half[:], 0.5)
        nc.scalar.activation(out=warm[:], in_=half[:], func=ACT.Abs_reciprocal_sqrt)
        rows = keep.tile([P, 512], BF16)
        nc.vector.memset(rows[:], 0.0)
        ident32 = keep.tile([P, P], F32)
        make_identity(nc, ident32[:])
        ident16 = keep.tile([P, P], BF16)
        make_identity(nc, ident16[:])

        x_sb = keep.tile([P, D], BF16)
        scale = keep.tile([P, PASSES, J], F32)

        units = []
        for r in range(RANGES):
            for i, (m, p) in enumerate(ORDER):
                units.append({"mat": m, "pass": p, "col": r, "engine": ENGINES[r][i]})
        for hh in range(HALVES):
            for p in range(GROUPS):
                units.append({"mat": 3, "pass": p, "col": hh, "engine": ENGINES[3][6 * hh + p]})
        total = len(units)
        for u in units:
            u["parts"] = [(0, W)]
        for u in (units[0], units[-1]):
            u["parts"] = [(0, W // 2), (W // 2, W)]

        def load(u):
            cols = slice(u["col"] * W, (u["col"] + 1) * W)
            p = u["pass"]
            if u["mat"] == 2:
                raw8 = raw8s.tile([P, J, W], U8, name="raw8")
                nc.sync.dma_start(
                    out=raw8[:], in_=w2_bytes[p * 512:(p + 1) * 512, cols].rearrange("(p k) c -> p k c", k=J))
                u["raw8"] = raw8
                return
            raw = raws.tile([P, J, W], BF16, name="raw")
            u["raw"] = raw
            if u["mat"] == 3:
                vrows = v[p * 512:(p + 1) * 512, cols].rearrange("(q t i) c -> i q t c", t=J, i=4)
                for i in range(4):
                    nc.sync.dma_start(out=raw[i::4, :, :], in_=vrows[i])
                return
            w = w1 if u["mat"] == 1 else w0
            src = w[p * 512:(p + 1) * 512, cols].rearrange("(p k) c -> p k c", k=J)
            for c0, c1 in u["parts"]:
                nc.sync.dma_start(out=raw[:, :, c0:c1], in_=src[:, :, c0:c1])

        def widen(u):
            wide = wides.tile([P, J, W], BF16, name="wide")
            for k in range(J):
                nc.scalar.activation(
                    out=wide[:, k, :], in_=u["raw8"][:, k, :].bitcast(FP8), func=ACT.Copy,
                    scale=scale[:, u["pass"], k:k + 1])
            u["raw"] = wide

        def turn(u, s):
            bank = psum.tile([P, 256, J], BF16, name="bank")
            u["banks"] = u.get("banks", []) + [bank]
            for h2 in range(2):
                c0 = 256 * s + 128 * h2
                nc.tensor.matmul(
                    bank[:, 128 * h2:128 * (h2 + 1), :], lhsT=ident16[:],
                    rhs=u["raw"][:, :, c0:c0 + 128].rearrange("p k c -> p c k"), start=True, stop=True)

        def unload(u, s):
            if s == 0:
                u["grp"] = grps.tile([P, J * W], BF16, name="grp", align_bytes=64)
            nc.scalar.copy(
                out=u["grp"][:, 1024 * s:1024 * (s + 1)], in_=u["banks"][s][:].rearrange("p c k -> p (c k)"))

        def interleave(u, engine):
            if "grp" not in u:
                u["grp"] = grps.tile([P, J * W], BF16, name="grp", align_bytes=64)
            grp = u["grp"]
            edge = W - 16 * SHARES[u["engine"]]
            for c0, c1 in u["parts"]:
                if engine == "S":
                    copy, c0, c1 = nc.scalar.copy, max(c0, edge), c1
                else:
                    copy, c0, c1 = nc.vector.tensor_copy, c0, min(c1, edge)
                if c0 >= c1:
                    continue
                if u["mat"] == 3:
                    dst = grp[:].rearrange("p (c i k) -> p c k i", i=4, k=J)[:, c0 // 4:c1 // 4]
                    src = u["raw"][:].rearrange("p k (c i) -> p c k i", i=4)[:, c0 // 4:c1 // 4]
                else:
                    dst = grp[:].rearrange("p (t q i k) -> p t q k i", t=4, i=4, k=J)[:, :, c0 // 16:c1 // 16]
                    src = u["raw"][:].rearrange("p k (q t i) -> p t q k i", t=4, i=4)[:, :, c0 // 16:c1 // 16]
                copy(out=dst, in_=src)

        def quantize(u):
            codes = qs.tile([P, W], U32, name="codes", align_bytes=64)
            planes = qs.tile([P, W], U8, name="planes", align_bytes=64)
            for c0, c1 in (u["parts"] if u["mat"] == 3 else [(0, W)]):
                nc.vector.quantize_mx(
                    out=codes[:, c0:c1].bitcast(FP8X4), scales=planes[:, c0:c1], in_=u["grp"][:, J * c0:J * c1])
            u["q"] = (codes, planes)

        words = x_sb[:].bitcast(F32)
        x_grp = keep.tile([P, PASSES, N, J], BF16, align_bytes=64)
        x_codes = keep.tile([P, PASSES, N], U32, align_bytes=64)
        x_planes = keep.tile([P, PASSES, N], U8, align_bytes=64)

        def prepare_x():
            x_words = x_grp[:].rearrange("p g n j -> p (g n j)").bitcast(F32).rearrange(
                "p (g n u) -> p g n u", g=PASSES, u=2)
            for h2 in range(2):
                bank = psum.tile([P, 2, 2, N], F32, name="bank")
                for gg in range(2):
                    for uu in range(2):
                        base = 256 * (2 * h2 + gg)
                        nc.tensor.transpose(bank[:, gg, uu, :], words[:, base + uu:base + 256:2], ident32[:])
                nc.vector.tensor_copy(
                    out=x_words[:, 2 * h2:2 * h2 + 2], in_=bank[:].rearrange("p g u n -> p g n u"))
            nc.vector.quantize_mx(
                out=x_codes[:].rearrange("p g n -> p (g n)").bitcast(FP8X4),
                scales=x_planes[:].rearrange("p g n -> p (g n)"),
                in_=x_grp[:].rearrange("p g n j -> p (g n j)"))

        col = keep.tile([P, 4, 32], F32)
        gb0 = keep.tile([P, 4, GROUPS], F32)
        rows_t = keep.tile([P, 4, 128], BF16)

        def load_rows():
            nc.sync.dma_start(out=rows[0:18, :], in_=b.rearrange("k (g c) -> (k g) c", c=512))
            nc.sync.dma_start(out=rows[18:24, :], in_=g.rearrange("(g c) -> g c", c=512))

        def prepare_rows():
            nc.vector.tensor_copy(
                out=rows_t[:].rearrange("p t (q i) -> p t q i", i=4),
                in_=rows[:].rearrange("p (q t i) -> p t q i", t=4, i=4))
            bank = psum.tile([P, 4, 128], BF16, name="bank")
            for t in range(4):
                nc.tensor.transpose(bank[:, t, :], rows_t[:, t, :], ident16[:])
            nc.vector.tensor_copy(out=col[:, :, 0:24], in_=bank[:, :, 0:24])
            nc.vector.tensor_tensor(out=gb0[:], in0=col[:, :, 0:6], in1=col[:, :, 18:24], op=ALU.mult)

        acc = {}
        ready = {}

        def first_matmuls(m, r):
            mine = [u for u in units if u["mat"] == m and u["col"] == r]
            mine.sort(key=lambda u: u["pass"])
            for gl in range(2):
                bank = psum.tile([P, 4, N], F32, name="bank")
                acc[(m, 2 * r + gl)] = bank
                for t in range(4):
                    c0 = t * 256 + gl * 128
                    for p in range(PASSES):
                        codes, planes = mine[p]["q"]
                        nc.tensor.matmul_mx(
                            out=bank[:, t, :],
                            lhsT=codes[:, c0:c0 + 128].bitcast(FP8X4), lhsT_scale=planes[:, c0:c0 + 128],
                            rhs=x_codes[:, p, :].bitcast(FP8X4), rhs_scale=x_planes[:, p, :],
                            start=(p == 0), stop=(p == PASSES - 1))

        st = {}

        def recip_half(src_sq, name):
            y = ep.tile([P, 4, N], F32, name="y")
            nc.scalar.activation(out=y[:], in_=src_sq[:], func=ACT.Abs_reciprocal_sqrt, bias=half[:])
            rec = ep.tile([P, 4, N], F32, name="rec")
            nc.scalar.activation(out=rec[:], in_=y[:], func=ACT.Square)
            return rec

        def e1_scalar(G):
            sq = ep.tile([P, 4, N], F32, name="sq")
            for t in range(4):
                nc.scalar.activation(
                    out=sq[:, t, :], in_=acc[(2, G)][:, t, :], func=ACT.Square, bias=col[:, t, 12 + G:13 + G])
            st[("rec", G)] = recip_half(sq, "a")

        def e1_vector(G):
            r2 = ep.tile([P, 4, N], F32, name="r2")
            for t in range(4):
                nc.vector.scalar_tensor_tensor(
                    out=r2[:, t, :], in0=acc[(2, G)][:, t, :], scalar=col[:, t, 12 + G:13 + G],
                    in1=st[("rec", G)][:, t, :], op0=ALU.add, op1=ALU.mult)
            st[("r2", G)] = r2

        def e2_vector(G):
            z1 = ep.tile([P, 4, N], F32, name="z1")
            for t in range(4):
                nc.vector.scalar_tensor_tensor(
                    out=z1[:, t, :], in0=acc[(1, G)][:, t, :], scalar=col[:, t, 6 + G:7 + G],
                    in1=st[("r2", G)][:, t, :], op0=ALU.add, op1=ALU.add)
            st[("z1", G)] = z1

        def e2_scalar(G):
            sq = ep.tile([P, 4, N], F32, name="sq")
            nc.scalar.activation(out=sq[:], in_=st[("z1", G)][:], func=ACT.Square)
            st[("rec1", G)] = recip_half(sq, "b")

        def e3_vector(G):
            gr = ep.tile([P, 4, N], F32, name="gr")
            for t in range(4):
                nc.vector.scalar_tensor_tensor(
                    out=gr[:, t, :], in0=st[("z1", G)][:, t, :], scalar=col[:, t, 18 + G:19 + G],
                    in1=st[("rec1", G)][:, t, :], op0=ALU.mult, op1=ALU.mult)
            st[("gr", G)] = gr

        def e4_scalar(G):
            z0 = ep.tile([P, 4, N], F32, name="z0")
            for t in range(4):
                nc.scalar.activation(
                    out=z0[:, t, :], in_=acc[(0, G)][:, t, :], func=ACT.Identity,
                    scale=col[:, t, 18 + G:19 + G], bias=gb0[:, t, G:G + 1])
            st[("z0", G)] = z0

        def e4_vector(G):
            hb = ep.tile([P, N, 4], BF16, name="hb", align_bytes=64)
            nc.vector.tensor_tensor(
                out=hb[:], in0=st[("z0", G)][:].rearrange("p t n -> p n t"),
                in1=st[("gr", G)][:].rearrange("p t n -> p n t"), op=ALU.add)
            st[("hb", G)] = hb

        h_codes = keep.tile([P, GROUPS, N], U32, align_bytes=64)
        h_planes = keep.tile([P, GROUPS, N], U8, align_bytes=64)

        def e5_vector(G):
            nc.vector.quantize_mx(
                out=h_codes[:, G, :].bitcast(FP8X4), scales=h_planes[:, G, :],
                in_=st[("hb", G)][:].rearrange("p n t -> p (n t)"))

        def last_matmuls(u):
            hh, G = u["col"], u["pass"]
            codes, planes = u["q"]
            for s in range(2):
                if G == 0:
                    bank = psum.tile([P, 512], F32, name="bank")
                    acc[("o", hh, s)] = bank
                nc.tensor.matmul_mx(
                    out=acc[("o", hh, s)][:],
                    lhsT=h_codes[:, G, :].bitcast(FP8X4), lhsT_scale=h_planes[:, G, :],
                    rhs=codes[:, 512 * s:512 * (s + 1)].bitcast(FP8X4), rhs_scale=planes[:, 512 * s:512 * (s + 1)],
                    start=(G == 0), stop=(G == GROUPS - 1))

        def finish(hh):
            for s in range(2):
                res = ep.tile([P, 512], F32, name="res")
                if s == 0:
                    nc.vector.tensor_copy(out=res[:], in_=acc[("o", hh, s)][:])
                else:
                    nc.scalar.copy(out=res[:], in_=acc[("o", hh, s)][:])
                c0 = hh * W + s * 512
                nc.sync.dma_start(out=out[:, c0:c0 + 512], in_=res[:])

        later = {}

        def at(step, fn, *args):
            later.setdefault(step, []).append((fn, args))

        def due(i, engine):
            return 0 <= i < total and units[i]["engine"] == engine

        done = {}
        pending = []
        ready_at = {}
        for s in range(-LOAD_LEAD, total + 8):
            if 0 <= s + LOAD_LEAD < total:
                load(units[s + LOAD_LEAD])
                if s + LOAD_LEAD == 1:
                    nc.sync.dma_start(out=scale[:], in_=w2_scale.rearrange("(g p k) o -> p g (k o)", p=P, k=J))
                    nc.sync.dma_start(out=x_sb[:], in_=x)
                if s + LOAD_LEAD == 4:
                    load_rows()
            if s == X_STEP:
                prepare_x()
            if s == X_STEP + 2:
                prepare_rows()
            if due(s + TURN_LEAD, "T"):
                for i in range(3):
                    turn(units[s + TURN_LEAD], i)
            if 0 <= s + WIDE_LEAD < total and units[s + WIDE_LEAD]["mat"] == 2:
                widen(units[s + WIDE_LEAD])
            if 0 <= s + S_LEAD < total and units[s + S_LEAD]["engine"] != "T":
                interleave(units[s + S_LEAD], "S")
            if due(s + TURN_LEAD - 1, "T"):
                u = units[s + TURN_LEAD - 1]
                unload(u, 0)
                turn(u, 3)
                for i in range(1, 4):
                    unload(u, i)
            if 0 <= s + 1 < total and units[s + 1]["engine"] != "T":
                interleave(units[s + 1], "V")
            if 0 <= s < total:
                u = units[s]
                quantize(u)
                m, r = u["mat"], u["col"]
                done[(m, r)] = done.get((m, r), 0) + 1
                if m == 3:
                    pending.append(u)
                elif done[(m, r)] == PASSES:
                    first_matmuls(m, r)
                    if m == 2:
                        for gl in range(2):
                            G = 2 * r + gl
                            base = s + gl
                            at(base + LAGS[0], e1_scalar, G)
                            at(base + LAGS[1], e1_vector, G)
                            at(base + LAGS[2], e2_vector, G)
                            at(base + LAGS[2], e2_scalar, G)
                            at(base + LAGS[3], e3_vector, G)
                            at(base + LAGS[4], e4_scalar, G)
                            at(base + LAGS[5], e4_vector, G)
                            at(base + LAGS[6], e5_vector, G)
                            ready_at[G] = base + LAGS[6]
            for fn, args in later.get(s, []):
                fn(*args)
            rest = []
            for u in pending:
                if ready_at[u["pass"]] <= s and not rest:
                    last_matmuls(u)
                    if u["pass"] == GROUPS - 1:
                        at(s + 1, finish, u["col"])
                else:
                    rest.append(u)
            pending = rest
